import numpy as np
import ml_dtypes


def mxq(x, axis, fmt="e4m3"):
    dtype, down = {"e4m3": (ml_dtypes.float8_e4m3fn, 7), "e5m2": (ml_dtypes.float8_e5m2, 14)}[fmt]
    v = np.moveaxis(np.asarray(x, np.float32).astype(ml_dtypes.bfloat16).astype(np.float64), axis, -1)
    blocks = v.reshape(v.shape[:-1] + (-1, 32))
    amax = np.abs(blocks).max(-1, keepdims=True)
    byte = np.maximum(np.where(amax > 0, np.frexp(amax)[1] - 1 + 127, 0) - down, 1)
    scale = np.exp2(byte - 127.0)
    codes = (blocks / scale).astype(np.float32).astype(dtype).astype(np.float64)
    return np.moveaxis((codes * scale).reshape(v.shape), -1, axis)


WIDE = False


def mx_kscale(k, group=512):
    if not WIDE:
        return np.ones(k)
    levels = np.array([18, -18])
    if group != 512:
        return np.exp2(np.random.permutation(np.resize(levels, k // group))).repeat(group)
    if k % 512:
        return np.exp2(np.random.permutation(np.resize(levels, k // 32))).repeat(32)
    a = np.empty((k // 512, 16))
    for p in range(k // 512):
        a[p, :8] = np.random.permutation(np.resize(levels, 8))
        for g in range(8):
            far = levels[np.abs(levels - a[p, g]) >= 10]
            a[p, g + 8] = far[np.random.randint(len(far))]
    return np.exp2(a.ravel()).repeat(32)


def f64(x):
    return np.asarray(x).astype(np.float64)


def sigmoid(v):
    return 1.0 / (1.0 + np.exp(-v))


G, D, M, O, N = 4, 128, 128, 128, 512


def sgn(shape):
    return np.random.uniform(0.5, 2.0, shape) * np.where(np.random.standard_normal(shape) < 0, -1.0, 1.0)


def setup_inputs():
    n = np.random.standard_normal
    s_d = mx_kscale(D, 0)
    s_m = mx_kscale(M, 0)
    return {
        "x": (n((G, D, N)) * s_d[:, None]).astype(np.float32),
        "w1": (n((G, D, M)) / np.sqrt(D) / s_d[:, None]).astype(np.float32),
        "w2": (n((G, D, M)) / np.sqrt(D) / s_d[:, None]).astype(np.float32),
        "tp": (np.random.uniform(0.5, 1.2, (G, M, 1))).astype(np.float32),
        "hs": (sgn((G, M, 1)) * s_m[:, None]).astype(np.float32),
        "wo2": (n((G, M, O)) / np.sqrt(M) / s_m[:, None]).astype(np.float32),
        "res": (0.5 * n((G, O, N))).astype(np.float32),
    }


def reference(x, w1, w2, tp, hs, wo2, res):
    w1q = mxq(f64(w1), 1, "e4m3")
    xq = mxq(f64(x), 1, "e4m3")
    z1 = w1q.transpose(0, 2, 1) @ xq
    w2q = mxq(f64(w2), 1, "e4m3")
    z2 = w2q.transpose(0, 2, 1) @ xq
    s1 = z1 * f64(tp)
    ls = np.log(np.sum(np.exp(s1), axis=-1, keepdims=True))
    h = (s1 - ls + 6.0) * sigmoid(z2)
    hh = h * f64(hs)
    wo2q = mxq(f64(wo2), 1, "e4m3")
    hhq = mxq(hh, 1, "e4m3")
    y0 = wo2q.transpose(0, 2, 1) @ hhq
    y = y0 + f64(res)
    return y

@@ -1,0 +1,207 @@
+import math
+from contextlib import ExitStack
+
+import concourse.mybir as mybir
+
+G, D, M, O, N = 4, 128, 128, 128, 512
+FLOPS = 2 * G * N * (2 * D * M + M * O)
+
+F32 = mybir.dt.float32
+BF16 = mybir.dt.bfloat16
+U32 = mybir.dt.uint32
+U8 = mybir.dt.uint8
+FP8X4 = mybir.dt.float8_e4m3fn_x4
+ALU = mybir.AluOpType
+ACT = mybir.ActivationFunctionType
+
+P = 128
+PACK = 4
+ROWS = 32
+HALF = N // 2
+STEPS = 16
+GUESS_SLOPE = math.log(2.0) / 2.0**23
+GUESS_SHIFT = 127.0 * math.log(2.0) - 0.03
+
+
+def tile_rows_frowlog_kernel(tc, x, w1, w2, tp, hs, wo2, res, out):
+    nc = tc.nc
+    with ExitStack() as ctx:
+        sb = ctx.enter_context(tc.tile_pool(name="sb", bufs=1))
+        ps = ctx.enter_context(tc.psum_pool(name="ps", bufs=1))
+        ctx.enter_context(tc.manual_schedule())
+
+        def rows(g):
+            return slice(ROWS * g, ROWS * (g + 1))
+
+        def packed(name, width):
+            words = sb.tile([P, width, PACK], BF16, name=name + "_words", align_bytes=64)
+            codes = sb.tile([P, width], U32, name=name + "_codes", align_bytes=64)
+            scales = sb.tile([P, width], U8, name=name + "_scales", align_bytes=64)
+            return words, codes, scales
+
+        def interleave(op, raw, raw0, col0, width, split):
+            words = op[0]
+            src = raw[:].rearrange("p j c -> p c j")
+            if split < width:
+                nc.scalar.activation(out=words[:, col0 + split : col0 + width, :],
+                                     in_=src[:, raw0 + split : raw0 + width, :], func=ACT.Copy)
+            if split > 0:
+                nc.vector.tensor_copy(out=words[:, col0 : col0 + split, :], in_=src[:, raw0 : raw0 + split, :])
+
+        def quantize(op, col0, width):
+            words, codes, scales = op
+            cols = slice(col0, col0 + width)
+            nc.vector.quantize_mx(out=codes[:, cols].bitcast(FP8X4), scales=scales[:, cols],
+                                  in_=words[:, cols, :].rearrange("p c j -> p (c j)"))
+
+        def product(acc, g, weights, moving):
+            nc.tensor.matmul_mx(out=acc[:], lhsT=weights[1][rows(g), :].bitcast(FP8X4), lhsT_scale=weights[2][rows(g), :],
+                                rhs=moving[1][rows(g), :].bitcast(FP8X4), rhs_scale=moving[2][rows(g), :],
+                                start=True, stop=True)
+
+        x_v = x.rearrange("g (p j) n -> (g p) j n", j=PACK)
+        x_raw = [sb.tile([P, PACK, HALF], F32, name="x_raw%d" % h) for h in range(2)]
+        w1_raw = sb.tile([P, PACK, M], F32)
+        w2_raw = sb.tile([P, PACK, M], F32)
+        wo_raw = sb.tile([P, PACK, O], F32)
+        res_sb = sb.tile([P, G, N], F32)
+        vec_rows = sb.tile([P, P], F32, align_bytes=64)
+        vec_cols = sb.tile([P, P], F32, align_bytes=64)
+        nc.vector.memset(vec_rows[:], 0.0)
+        for h in range(2):
+            nc.sync.dma_start(out=x_raw[h][:], in_=x_v[:, :, HALF * h : HALF * (h + 1)])
+        nc.sync.dma_start(out=w1_raw[:], in_=w1.rearrange("g (p j) m -> (g p) j m", j=PACK))
+        nc.sync.dma_start(out=w2_raw[:], in_=w2.rearrange("g (p j) m -> (g p) j m", j=PACK))
+        nc.sync.dma_start(out=wo_raw[:], in_=wo2.rearrange("g (p j) o -> (g p) j o", j=PACK))
+        nc.sync.dma_start(out=res_sb[:], in_=res.rearrange("g o n -> o g n"))
+        for r, vec in enumerate((tp, hs)):
+            nc.scalar.dma_start(out=vec_rows[r:P:ROWS, :].rearrange("q (g c) -> q g c", g=G),
+                                in_=vec.rearrange("g (q c) o -> q g (c o)", c=ROWS))
+
+        delta = sb.tile([P, G, STEPS], F32)
+        coef = sb.tile([P, G, STEPS], F32)
+        nc.vector.memset(delta[:, :, 0:1], 0.0)
+        odd = sb.tile([P, STEPS // 2], F32)
+        even = sb.tile([P, STEPS // 2 - 1], F32)
+        nc.gpsimd.iota(odd[:], [[-2, STEPS // 2]], base=STEPS - 1, channel_multiplier=0,
+                       allow_small_or_imprecise_dtypes=True)
+        nc.gpsimd.iota(even[:], [[2, STEPS // 2 - 1]], base=2 - STEPS, channel_multiplier=0,
+                       allow_small_or_imprecise_dtypes=True)
+        nc.vector.reciprocal(out=coef[:, :, 0:STEPS:2], in_=odd[:].unsqueeze(1).to_broadcast([P, G, STEPS // 2]))
+        nc.vector.reciprocal(out=coef[:, :, 1 : STEPS - 2 : 2], in_=even[:].unsqueeze(1).to_broadcast([P, G, STEPS // 2 - 1]))
+
+        xq = packed("x", N)
+        w1q = packed("w1", M)
+        w2q = packed("w2", M)
+        woq = packed("wo", O)
+        hq = packed("h", N)
+
+        interleave(xq, x_raw[0], 0, 0, HALF, 168)
+        nc.vector.transpose(out=vec_cols[:], in_=vec_rows[:])
+        quantize(xq, 0, HALF)
+        neg_tp = sb.tile([P, G], F32)
+        neg_half_hs = sb.tile([P, G], F32)
+        nc.vector.tensor_scalar(out=neg_tp[:], in0=vec_cols[:, 0:P:ROWS], scalar1=-1.0, scalar2=None, op0=ALU.mult)
+        nc.vector.tensor_scalar(out=neg_half_hs[:], in0=vec_cols[:, 1:P:ROWS], scalar1=-0.5, scalar2=None, op0=ALU.mult)
+        interleave(xq, x_raw[1], 0, HALF, HALF, 168)
+        quantize(xq, HALF, HALF)
+        interleave(w1q, w1_raw, 0, 0, M, 64)
+        quantize(w1q, 0, M)
+        z1 = [ps.tile([P, N], F32, name="z1_%d" % g) for g in range(G)]
+        z2 = [ps.tile([P, N], F32, name="z2_%d" % g) for g in range(G)]
+        for g in range(G):
+            product(z1[g], g, w1q, xq)
+        interleave(w2q, w2_raw, 0, 0, M, 64)
+        quantize(w2q, 0, M)
+        for g in range(G):
+            product(z2[g], g, w2q, xq)
+
+        neg_s = [sb.tile([P, N], F32, name="neg_s%d" % g) for g in range(G)]
+        th = [sb.tile([P, N], F32, name="th%d" % g) for g in range(G)]
+        gate = [sb.tile([P, N], F32, name="gate%d" % g) for g in range(G)]
+        ex = [sb.tile([P, N], BF16, name="ex%d" % g) for g in range(G)]
+        hh = [sb.tile([P, N], BF16, name="hh%d" % g) for g in range(G)]
+        neg_max = sb.tile([P, G], F32)
+        total = sb.tile([P, G], F32)
+        guess = sb.tile([P, G], F32)
+        inv = sb.tile([P, G], F32)
+        shift = sb.tile([P, G, STEPS], F32)
+        h_raw = sb.tile([P, PACK, N], BF16)
+
+        def scores(g):
+            nc.vector.tensor_scalar(out=neg_s[g][:], in0=z1[g][:], scalar1=neg_tp[:, g : g + 1], scalar2=None,
+                                    op0=ALU.mult, op1=ALU.min, accum_out=neg_max[:, g : g + 1])
+
+        def exps(g):
+            nc.scalar.activation(out=ex[g][:], in_=neg_s[g][:], func=ACT.Exp, scale=-1.0, bias=neg_max[:, g : g + 1],
+                                 accum_out=total[:, g : g + 1])
+
+        def tanh(g):
+            nc.scalar.activation(out=th[g][:], in_=z2[g][:], func=ACT.Tanh, scale=0.5)
+
+        def gates(g):
+            nc.vector.tensor_scalar(out=gate[g][:], in0=th[g][:], scalar1=1.0, scalar2=neg_half_hs[:, g : g + 1],
+                                    op0=ALU.add, op1=ALU.mult)
+
+        def log_guess(g0, g1):
+            bits = total[:, g0:g1].bitcast(U32)
+            nc.scalar.activation(out=inv[:, g0:g1], in_=bits, func=ACT.Exp, scale=-GUESS_SLOPE, bias=GUESS_SHIFT)
+            nc.scalar.activation(out=guess[:, g0:g1], in_=bits, func=ACT.Copy, scale=GUESS_SLOPE, bias=-GUESS_SHIFT)
+
+        def log_delta(g0, g1):
+            for g in range(g0, g1):
+                nc.vector.tensor_scalar(out=delta[:, g, 1:STEPS], in0=total[:, g : g + 1].to_broadcast([P, STEPS - 1]),
+                                        scalar1=inv[:, g : g + 1], scalar2=-1.0, op0=ALU.mult, op1=ALU.add)
+            nc.vector.scalar_tensor_tensor(out=coef[:, g0:g1, STEPS - 1], in0=guess[:, g0:g1], scalar=-6.0,
+                                           in1=neg_max[:, g0:g1], op0=ALU.add, op1=ALU.subtract)
+
+        def log_series(g0, g1):
+            flat = "p g s -> p (g s)"
+            nc.vector.tensor_tensor_scan(out=shift[:, g0:g1, :].rearrange(flat), data0=delta[:, g0:g1, :].rearrange(flat),
+                                         data1=coef[:, g0:g1, :].rearrange(flat), initial=0.0, op0=ALU.mult, op1=ALU.add)
+
+        def hidden(g, c0, c1):
+            nc.vector.scalar_tensor_tensor(out=hh[g][:, c0:c1], in0=neg_s[g][:, c0:c1], scalar=shift[:, g, STEPS - 1 : STEPS],
+                                           in1=gate[g][:, c0:c1], op0=ALU.add, op1=ALU.mult)
+            nc.sync.dma_start(out=h_raw[rows(g), :, c0:c1], in_=hh[g][:, c0:c1])
+
+        for g in range(G):
+            scores(g)
+        exps(0)
+        exps(1)
+        tanh(0)
+        log_guess(0, 2)
+        exps(2)
+        exps(3)
+        tanh(1)
+        log_guess(2, 4)
+        tanh(2)
+        tanh(3)
+        interleave(woq, wo_raw, 0, 0, O, 0)
+
+        log_delta(0, 2)
+        gates(0)
+        log_series(0, 2)
+        hidden(0, 0, N)
+        gates(1)
+        log_delta(2, 4)
+        hidden(1, 0, N)
+        log_series(2, 4)
+        gates(2)
+        hidden(2, 0, HALF)
+        gates(3)
+        hidden(3, 0, HALF)
+        hidden(2, HALF, N)
+        hidden(3, HALF, N)
+        quantize(woq, 0, O)
+
+        for h in range(2):
+            interleave(hq, h_raw, HALF * h, HALF * h, HALF, 168)
+            quantize(hq, HALF * h, HALF)
+        y = [ps.tile([P, N], F32, name="z1_%d" % g) for g in range(G)]
+        result = [sb.tile([P, N], F32, name="result%d" % g) for g in range(G)]
+        for g in range(G):
+            product(y[g], g, woq, hq)
+        for g in range(G):
+            nc.vector.tensor_tensor(out=result[g][:], in0=y[g][:], in1=res_sb[:, g, :], op=ALU.add)
+            nc.sync.dma_start(out=out[g], in_=result[g][:])

@@ -18,6 +18,7 @@ P = 128
 PACK = 4
 ROWS = 32
 HALF = N // 2
+RUN = 4
 STEPS = 16
 GUESS_SLOPE = math.log(2.0) / 2.0**23
 GUESS_SHIFT = 127.0 * math.log(2.0) - 0.03
@@ -40,13 +41,12 @@ def tile_rows_frowlog_kernel(tc, x, w1, w2, tp, hs, wo2, res, out):
             return words, codes, scales
 
         def interleave(op, raw, raw0, col0, width, split):
-            words = op[0]
-            src = raw[:].rearrange("p j c -> p c j")
+            dst = op[0][:, col0 : col0 + width, :].rearrange("p (c i) j -> p c j i", i=RUN)
+            src = raw[:, :, raw0 : raw0 + width].rearrange("p j (c i) -> p c j i", i=RUN)
             if split < width:
-                nc.scalar.activation(out=words[:, col0 + split : col0 + width, :],
-                                     in_=src[:, raw0 + split : raw0 + width, :], func=ACT.Copy)
+                nc.scalar.activation(out=dst[:, split // RUN :], in_=src[:, split // RUN :], func=ACT.Copy)
             if split > 0:
-                nc.vector.tensor_copy(out=words[:, col0 : col0 + split, :], in_=src[:, raw0 : raw0 + split, :])
+                nc.vector.tensor_copy(out=dst[:, : split // RUN], in_=src[:, : split // RUN])
 
         def quantize(op, col0, width):
             words, codes, scales = op
@@ -67,16 +67,16 @@ def tile_rows_frowlog_kernel(tc, x, w1, w2, tp, hs, wo2, res, out):
         res_sb = sb.tile([P, G, N], F32)
         vec_rows = sb.tile([P, P], F32, align_bytes=64)
         vec_cols = sb.tile([P, P], F32, align_bytes=64)
-        nc.vector.memset(vec_rows[:], 0.0)
-        for h in range(2):
-            nc.sync.dma_start(out=x_raw[h][:], in_=x_v[:, :, HALF * h : HALF * (h + 1)])
+        nc.gpsimd.memset(vec_rows[:], 0.0)
+        nc.sync.dma_start(out=x_raw[0][:], in_=x_v[:, :, 0:HALF])
+        for r, vec in enumerate((tp, hs)):
+            nc.sync.dma_start(out=vec_rows[r:P:ROWS, :].rearrange("q (g c) -> q g c", g=G),
+                              in_=vec.rearrange("g (q c) o -> q g (c o)", c=ROWS))
+        nc.sync.dma_start(out=x_raw[1][:], in_=x_v[:, :, HALF:N])
         nc.sync.dma_start(out=w1_raw[:], in_=w1.rearrange("g (p j) m -> (g p) j m", j=PACK))
         nc.sync.dma_start(out=w2_raw[:], in_=w2.rearrange("g (p j) m -> (g p) j m", j=PACK))
         nc.sync.dma_start(out=wo_raw[:], in_=wo2.rearrange("g (p j) o -> (g p) j o", j=PACK))
         nc.sync.dma_start(out=res_sb[:], in_=res.rearrange("g o n -> o g n"))
-        for r, vec in enumerate((tp, hs)):
-            nc.scalar.dma_start(out=vec_rows[r:P:ROWS, :].rearrange("q (g c) -> q g c", g=G),
-                                in_=vec.rearrange("g (q c) o -> q g (c o)", c=ROWS))
 
         delta = sb.tile([P, G, STEPS], F32)
         coef = sb.tile([P, G, STEPS], F32)
@@ -109,12 +109,14 @@ def tile_rows_frowlog_kernel(tc, x, w1, w2, tp, hs, wo2, res, out):
         quantize(w1q, 0, M)
         z1 = [ps.tile([P, N], F32, name="z1_%d" % g) for g in range(G)]
         z2 = [ps.tile([P, N], F32, name="z2_%d" % g) for g in range(G)]
-        for g in range(G):
-            product(z1[g], g, w1q, xq)
+        product(z1[0], 0, w1q, xq)
+        product(z1[1], 1, w1q, xq)
         interleave(w2q, w2_raw, 0, 0, M, 64)
         quantize(w2q, 0, M)
         for g in range(G):
             product(z2[g], g, w2q, xq)
+            if g + 2 < G:
+                product(z1[g + 2], g + 2, w1q, xq)
 
         neg_s = [sb.tile([P, N], F32, name="neg_s%d" % g) for g in range(G)]
         th = [sb.tile([P, N], F32, name="th%d" % g) for g in range(G)]
@@ -167,36 +169,36 @@ def tile_rows_frowlog_kernel(tc, x, w1, w2, tp, hs, wo2, res, out):
 
         for g in range(G):
             scores(g)
+        tanh(0)
         exps(0)
         exps(1)
-        tanh(0)
+        tanh(1)
         log_guess(0, 2)
         exps(2)
         exps(3)
-        tanh(1)
-        log_guess(2, 4)
         tanh(2)
+        log_guess(2, 4)
         tanh(3)
         interleave(woq, wo_raw, 0, 0, O, 0)
 
-        log_delta(0, 2)
         gates(0)
+        log_delta(0, 2)
+        gates(1)
         log_series(0, 2)
         hidden(0, 0, N)
-        gates(1)
-        log_delta(2, 4)
         hidden(1, 0, N)
-        log_series(2, 4)
+        log_delta(2, 4)
         gates(2)
-        hidden(2, 0, HALF)
+        log_series(2, 4)
         gates(3)
+        hidden(2, 0, HALF)
         hidden(3, 0, HALF)
         hidden(2, HALF, N)
         hidden(3, HALF, N)
         quantize(woq, 0, O)
 
         for h in range(2):
-            interleave(hq, h_raw, HALF * h, HALF * h, HALF, 168)
+            interleave(hq, h_raw, HALF * h, HALF * h, HALF, (168, 128)[h])
             quantize(hq, HALF * h, HALF)
         y = [ps.tile([P, N], F32, name="z1_%d" % g) for g in range(G)]
         result = [sb.tile([P, N], F32, name="result%d" % g) for g in range(G)]

@@ -19,6 +19,7 @@ PACK = 4
 ROWS = 32
 HALF = N // 2
 RUN = 4
+WIDTH = 128
 STEPS = 16
 GUESS_SLOPE = math.log(2.0) / 2.0**23
 GUESS_SHIFT = 127.0 * math.log(2.0) - 0.03
@@ -54,10 +55,12 @@ def tile_rows_frowlog_kernel(tc, x, w1, w2, tp, hs, wo2, res, out):
             nc.vector.quantize_mx(out=codes[:, cols].bitcast(FP8X4), scales=scales[:, cols],
                                   in_=words[:, cols, :].rearrange("p c j -> p (c j)"))
 
-        def product(acc, g, weights, moving):
-            nc.tensor.matmul_mx(out=acc[:], lhsT=weights[1][rows(g), :].bitcast(FP8X4), lhsT_scale=weights[2][rows(g), :],
-                                rhs=moving[1][rows(g), :].bitcast(FP8X4), rhs_scale=moving[2][rows(g), :],
-                                start=True, stop=True)
+        def product(acc, g, weights, moving, c0, c1):
+            for c in range(c0, c1, WIDTH):
+                cols = slice(c, c + WIDTH)
+                nc.tensor.matmul_mx(out=acc[:, cols], lhsT=weights[1][rows(g), :].bitcast(FP8X4),
+                                    lhsT_scale=weights[2][rows(g), :], rhs=moving[1][rows(g), cols].bitcast(FP8X4),
+                                    rhs_scale=moving[2][rows(g), cols], start=True, stop=True)
 
         x_v = x.rearrange("g (p j) n -> (g p) j n", j=PACK)
         x_raw = [sb.tile([P, PACK, HALF], F32, name="x_raw%d" % h) for h in range(2)]
@@ -72,8 +75,8 @@ def tile_rows_frowlog_kernel(tc, x, w1, w2, tp, hs, wo2, res, out):
         for r, vec in enumerate((tp, hs)):
             nc.sync.dma_start(out=vec_rows[r:P:ROWS, :].rearrange("q (g c) -> q g c", g=G),
                               in_=vec.rearrange("g (q c) o -> q g (c o)", c=ROWS))
-        nc.sync.dma_start(out=x_raw[1][:], in_=x_v[:, :, HALF:N])
         nc.sync.dma_start(out=w1_raw[:], in_=w1.rearrange("g (p j) m -> (g p) j m", j=PACK))
+        nc.sync.dma_start(out=x_raw[1][:], in_=x_v[:, :, HALF:N])
         nc.sync.dma_start(out=w2_raw[:], in_=w2.rearrange("g (p j) m -> (g p) j m", j=PACK))
         nc.sync.dma_start(out=wo_raw[:], in_=wo2.rearrange("g (p j) o -> (g p) j o", j=PACK))
         nc.sync.dma_start(out=res_sb[:], in_=res.rearrange("g o n -> o g n"))
@@ -96,27 +99,29 @@ def tile_rows_frowlog_kernel(tc, x, w1, w2, tp, hs, wo2, res, out):
         woq = packed("wo", O)
         hq = packed("h", N)
 
+        neg_tp = sb.tile([P, G], F32)
+        neg_half_hs = sb.tile([P, G], F32)
+        z1 = [ps.tile([P, N], F32, name="z1_%d" % g) for g in range(G)]
+        z2 = [ps.tile([P, N], F32, name="z2_%d" % g) for g in range(G)]
         interleave(xq, x_raw[0], 0, 0, HALF, 168)
         nc.vector.transpose(out=vec_cols[:], in_=vec_rows[:])
         quantize(xq, 0, HALF)
-        neg_tp = sb.tile([P, G], F32)
-        neg_half_hs = sb.tile([P, G], F32)
+        interleave(w1q, w1_raw, 0, 0, M, 64)
         nc.vector.tensor_scalar(out=neg_tp[:], in0=vec_cols[:, 0:P:ROWS], scalar1=-1.0, scalar2=None, op0=ALU.mult)
         nc.vector.tensor_scalar(out=neg_half_hs[:], in0=vec_cols[:, 1:P:ROWS], scalar1=-0.5, scalar2=None, op0=ALU.mult)
+        quantize(w1q, 0, M)
+        for g in range(G):
+            product(z1[g], g, w1q, xq, 0, HALF)
         interleave(xq, x_raw[1], 0, HALF, HALF, 168)
         quantize(xq, HALF, HALF)
-        interleave(w1q, w1_raw, 0, 0, M, 64)
-        quantize(w1q, 0, M)
-        z1 = [ps.tile([P, N], F32, name="z1_%d" % g) for g in range(G)]
-        z2 = [ps.tile([P, N], F32, name="z2_%d" % g) for g in range(G)]
-        product(z1[0], 0, w1q, xq)
-        product(z1[1], 1, w1q, xq)
+        product(z1[0], 0, w1q, xq, HALF, N)
+        product(z1[1], 1, w1q, xq, HALF, N)
         interleave(w2q, w2_raw, 0, 0, M, 64)
         quantize(w2q, 0, M)
         for g in range(G):
-            product(z2[g], g, w2q, xq)
+            product(z2[g], g, w2q, xq, 0, N)
             if g + 2 < G:
-                product(z1[g + 2], g + 2, w1q, xq)
+                product(z1[g + 2], g + 2, w1q, xq, HALF, N)
 
         neg_s = [sb.tile([P, N], F32, name="neg_s%d" % g) for g in range(G)]
         th = [sb.tile([P, N], F32, name="th%d" % g) for g in range(G)]
@@ -191,19 +196,23 @@ def tile_rows_frowlog_kernel(tc, x, w1, w2, tp, hs, wo2, res, out):
         gates(2)
         log_series(2, 4)
         gates(3)
-        hidden(2, 0, HALF)
-        hidden(3, 0, HALF)
-        hidden(2, HALF, N)
-        hidden(3, HALF, N)
+        for c0 in (0, HALF):
+            hidden(2, c0, c0 + HALF)
+            hidden(3, c0, c0 + HALF)
         quantize(woq, 0, O)
 
-        for h in range(2):
-            interleave(hq, h_raw, HALF * h, HALF * h, HALF, (168, 128)[h])
-            quantize(hq, HALF * h, HALF)
-        y = [ps.tile([P, N], F32, name="z1_%d" % g) for g in range(G)]
+        y = {}
+        for g in range(G):
+            y[g, 0] = ps.tile([P, N], F32, name="z1_%d" % g)
+            y[g, HALF] = ps.tile([P, N], F32, name="z2_%d" % g)
         result = [sb.tile([P, N], F32, name="result%d" % g) for g in range(G)]
-        for g in range(G):
-            product(y[g], g, woq, hq)
-        for g in range(G):
-            nc.vector.tensor_tensor(out=result[g][:], in0=y[g][:], in1=res_sb[:, g, :], op=ALU.add)
-            nc.sync.dma_start(out=out[g], in_=result[g][:])
+        for c0 in (0, HALF):
+            interleave(hq, h_raw, c0, c0, HALF, 96 if c0 else 168)
+            quantize(hq, c0, HALF)
+            for g in range(G):
+                product(y[g, c0], g, woq, hq, c0, c0 + HALF)
+        for c0 in (0, HALF):
+            cols = slice(c0, c0 + HALF)
+            for g in range(G):
+                nc.vector.tensor_tensor(out=result[g][:, cols], in0=y[g, c0][:, cols], in1=res_sb[:, g, cols], op=ALU.add)
+                nc.sync.dma_start(out=out[g, :, cols], in_=result[g][:, cols])

@@ -55,12 +55,13 @@ def tile_rows_frowlog_kernel(tc, x, w1, w2, tp, hs, wo2, res, out):
             nc.vector.quantize_mx(out=codes[:, cols].bitcast(FP8X4), scales=scales[:, cols],
                                   in_=words[:, cols, :].rearrange("p c j -> p (c j)"))
 
-        def product(acc, g, weights, moving, c0, c1):
+        def products(acc, groups, weights, moving, c0, c1):
             for c in range(c0, c1, WIDTH):
                 cols = slice(c, c + WIDTH)
-                nc.tensor.matmul_mx(out=acc[:, cols], lhsT=weights[1][rows(g), :].bitcast(FP8X4),
-                                    lhsT_scale=weights[2][rows(g), :], rhs=moving[1][rows(g), cols].bitcast(FP8X4),
-                                    rhs_scale=moving[2][rows(g), cols], start=True, stop=True)
+                for g in groups:
+                    nc.tensor.matmul_mx(out=acc[g][:, cols], lhsT=weights[1][rows(g), :].bitcast(FP8X4),
+                                        lhsT_scale=weights[2][rows(g), :], rhs=moving[1][rows(g), cols].bitcast(FP8X4),
+                                        rhs_scale=moving[2][rows(g), cols], start=True, stop=True)
 
         x_v = x.rearrange("g (p j) n -> (g p) j n", j=PACK)
         x_raw = [sb.tile([P, PACK, HALF], F32, name="x_raw%d" % h) for h in range(2)]
@@ -70,7 +71,7 @@ def tile_rows_frowlog_kernel(tc, x, w1, w2, tp, hs, wo2, res, out):
         res_sb = sb.tile([P, G, N], F32)
         vec_rows = sb.tile([P, P], F32, align_bytes=64)
         vec_cols = sb.tile([P, P], F32, align_bytes=64)
-        nc.gpsimd.memset(vec_rows[:], 0.0)
+        nc.vector.memset(vec_rows[:], 0.0)
         nc.sync.dma_start(out=x_raw[0][:], in_=x_v[:, :, 0:HALF])
         for r, vec in enumerate((tp, hs)):
             nc.sync.dma_start(out=vec_rows[r:P:ROWS, :].rearrange("q (g c) -> q g c", g=G),
@@ -84,14 +85,9 @@ def tile_rows_frowlog_kernel(tc, x, w1, w2, tp, hs, wo2, res, out):
         delta = sb.tile([P, G, STEPS], F32)
         coef = sb.tile([P, G, STEPS], F32)
         nc.vector.memset(delta[:, :, 0:1], 0.0)
-        odd = sb.tile([P, STEPS // 2], F32)
-        even = sb.tile([P, STEPS // 2 - 1], F32)
-        nc.gpsimd.iota(odd[:], [[-2, STEPS // 2]], base=STEPS - 1, channel_multiplier=0,
-                       allow_small_or_imprecise_dtypes=True)
-        nc.gpsimd.iota(even[:], [[2, STEPS // 2 - 1]], base=2 - STEPS, channel_multiplier=0,
-                       allow_small_or_imprecise_dtypes=True)
-        nc.vector.reciprocal(out=coef[:, :, 0:STEPS:2], in_=odd[:].unsqueeze(1).to_broadcast([P, G, STEPS // 2]))
-        nc.vector.reciprocal(out=coef[:, :, 1 : STEPS - 2 : 2], in_=even[:].unsqueeze(1).to_broadcast([P, G, STEPS // 2 - 1]))
+        for k in range(STEPS - 1):
+            nc.vector.tensor_scalar(out=coef[:, :, k : k + 1], in0=delta[:, :, 0:1], scalar1=(-1.0) ** k / (STEPS - 1 - k),
+                                    scalar2=None, op0=ALU.add)
 
         xq = packed("x", N)
         w1q = packed("w1", M)
@@ -103,25 +99,6 @@ def tile_rows_frowlog_kernel(tc, x, w1, w2, tp, hs, wo2, res, out):
         neg_half_hs = sb.tile([P, G], F32)
         z1 = [ps.tile([P, N], F32, name="z1_%d" % g) for g in range(G)]
         z2 = [ps.tile([P, N], F32, name="z2_%d" % g) for g in range(G)]
-        interleave(xq, x_raw[0], 0, 0, HALF, 168)
-        nc.vector.transpose(out=vec_cols[:], in_=vec_rows[:])
-        quantize(xq, 0, HALF)
-        interleave(w1q, w1_raw, 0, 0, M, 64)
-        nc.vector.tensor_scalar(out=neg_tp[:], in0=vec_cols[:, 0:P:ROWS], scalar1=-1.0, scalar2=None, op0=ALU.mult)
-        nc.vector.tensor_scalar(out=neg_half_hs[:], in0=vec_cols[:, 1:P:ROWS], scalar1=-0.5, scalar2=None, op0=ALU.mult)
-        quantize(w1q, 0, M)
-        for g in range(G):
-            product(z1[g], g, w1q, xq, 0, HALF)
-        interleave(xq, x_raw[1], 0, HALF, HALF, 168)
-        quantize(xq, HALF, HALF)
-        product(z1[0], 0, w1q, xq, HALF, N)
-        product(z1[1], 1, w1q, xq, HALF, N)
-        interleave(w2q, w2_raw, 0, 0, M, 64)
-        quantize(w2q, 0, M)
-        for g in range(G):
-            product(z2[g], g, w2q, xq, 0, N)
-            if g + 2 < G:
-                product(z1[g + 2], g + 2, w1q, xq, HALF, N)
 
         neg_s = [sb.tile([P, N], F32, name="neg_s%d" % g) for g in range(G)]
         th = [sb.tile([P, N], F32, name="th%d" % g) for g in range(G)]
@@ -129,15 +106,16 @@ def tile_rows_frowlog_kernel(tc, x, w1, w2, tp, hs, wo2, res, out):
         ex = [sb.tile([P, N], BF16, name="ex%d" % g) for g in range(G)]
         hh = [sb.tile([P, N], BF16, name="hh%d" % g) for g in range(G)]
         neg_max = sb.tile([P, G], F32)
+        half_max = sb.tile([P, 2], F32)
         total = sb.tile([P, G], F32)
         guess = sb.tile([P, G], F32)
         inv = sb.tile([P, G], F32)
         shift = sb.tile([P, G, STEPS], F32)
         h_raw = sb.tile([P, PACK, N], BF16)
 
-        def scores(g):
-            nc.vector.tensor_scalar(out=neg_s[g][:], in0=z1[g][:], scalar1=neg_tp[:, g : g + 1], scalar2=None,
-                                    op0=ALU.mult, op1=ALU.min, accum_out=neg_max[:, g : g + 1])
+        def scores(g, c0, c1, so_far, minimum):
+            nc.vector.tensor_scalar(out=neg_s[g][:, c0:c1], in0=z1[g][:, c0:c1], scalar1=neg_tp[:, g : g + 1], scalar2=so_far,
+                                    op0=ALU.mult, op1=ALU.min, accum_out=minimum[:, g : g + 1])
 
         def exps(g):
             nc.scalar.activation(out=ex[g][:], in_=neg_s[g][:], func=ACT.Exp, scale=-1.0, bias=neg_max[:, g : g + 1],
@@ -172,13 +150,34 @@ def tile_rows_frowlog_kernel(tc, x, w1, w2, tp, hs, wo2, res, out):
                                            in1=gate[g][:, c0:c1], op0=ALU.add, op1=ALU.mult)
             nc.sync.dma_start(out=h_raw[rows(g), :, c0:c1], in_=hh[g][:, c0:c1])
 
-        for g in range(G):
-            scores(g)
-        tanh(0)
+        interleave(xq, x_raw[0], 0, 0, HALF, 168)
+        quantize(xq, 0, HALF)
+        interleave(w1q, w1_raw, 0, 0, M, 64)
+        nc.vector.transpose(out=vec_cols[:], in_=vec_rows[:])
+        quantize(w1q, 0, M)
+        nc.vector.tensor_scalar(out=neg_tp[:], in0=vec_cols[:, 0:P:ROWS], scalar1=-1.0, scalar2=None, op0=ALU.mult)
+        nc.vector.tensor_scalar(out=neg_half_hs[:], in0=vec_cols[:, 1:P:ROWS], scalar1=-0.5, scalar2=None, op0=ALU.mult)
+        products(z1, (0, 1), w1q, xq, 0, HALF)
+        products(z1, (2, 3), w1q, xq, 0, HALF)
+        interleave(xq, x_raw[1], 0, HALF, HALF, 168)
+        scores(0, 0, HALF, None, half_max)
+        quantize(xq, HALF, HALF)
+        interleave(w2q, w2_raw, 0, 0, M, 64)
+        scores(1, 0, HALF, None, half_max)
+        quantize(w2q, 0, M)
+        products(z1, (0, 2), w1q, xq, HALF, N)
+        products(z1, (1, 3), w1q, xq, HALF, N)
+        products(z2, (0, 1), w2q, xq, 0, N)
+        products(z2, (2, 3), w2q, xq, 0, N)
+        for g in range(2):
+            scores(g, HALF, N, half_max[:, g : g + 1], neg_max)
+        for g in range(2, G):
+            scores(g, 0, N, None, neg_max)
         exps(0)
         exps(1)
-        tanh(1)
+        tanh(0)
         log_guess(0, 2)
+        tanh(1)
         exps(2)
         exps(3)
         tanh(2)
@@ -201,18 +200,16 @@ def tile_rows_frowlog_kernel(tc, x, w1, w2, tp, hs, wo2, res, out):
             hidden(3, c0, c0 + HALF)
         quantize(woq, 0, O)
 
-        y = {}
-        for g in range(G):
-            y[g, 0] = ps.tile([P, N], F32, name="z1_%d" % g)
-            y[g, HALF] = ps.tile([P, N], F32, name="z2_%d" % g)
+        y = {0: [ps.tile([P, N], F32, name="z1_%d" % g) for g in range(G)],
+             HALF: [ps.tile([P, N], F32, name="z2_%d" % g) for g in range(G)]}
         result = [sb.tile([P, N], F32, name="result%d" % g) for g in range(G)]
         for c0 in (0, HALF):
             interleave(hq, h_raw, c0, c0, HALF, 96 if c0 else 168)
             quantize(hq, c0, HALF)
-            for g in range(G):
-                product(y[g, c0], g, woq, hq, c0, c0 + HALF)
+            products(y[c0], (0, 1), woq, hq, c0, c0 + HALF)
+            products(y[c0], (2, 3), woq, hq, c0, c0 + HALF)
         for c0 in (0, HALF):
             cols = slice(c0, c0 + HALF)
             for g in range(G):
-                nc.vector.tensor_tensor(out=result[g][:, cols], in0=y[g, c0][:, cols], in1=res_sb[:, g, cols], op=ALU.add)
+                nc.vector.tensor_tensor(out=result[g][:, cols], in0=y[c0][g][:, cols], in1=res_sb[:, g, cols], op=ALU.add)
                 nc.sync.dma_start(out=out[g, :, cols], in_=result[g][:, cols])

import math
from contextlib import ExitStack

import concourse.mybir as mybir

G, D, M, O, N = 4, 128, 128, 128, 512
FLOPS = 2 * G * N * (2 * D * M + M * O)

F32 = mybir.dt.float32
BF16 = mybir.dt.bfloat16
U32 = mybir.dt.uint32
U8 = mybir.dt.uint8
FP8X4 = mybir.dt.float8_e4m3fn_x4
ALU = mybir.AluOpType
ACT = mybir.ActivationFunctionType

P = 128
PACK = 4
ROWS = 32
HALF = N // 2
RUN = 4
WIDTH = 128
STEPS = 16
GUESS_SLOPE = math.log(2.0) / 2.0**23
GUESS_SHIFT = 127.0 * math.log(2.0) - 0.03


def tile_rows_frowlog_kernel(tc, x, w1, w2, tp, hs, wo2, res, out):
    nc = tc.nc
    with ExitStack() as ctx:
        sb = ctx.enter_context(tc.tile_pool(name="sb", bufs=1))
        ps = ctx.enter_context(tc.psum_pool(name="ps", bufs=1))
        ctx.enter_context(tc.manual_schedule())

        def rows(g):
            return slice(ROWS * g, ROWS * (g + 1))

        def packed(name, width):
            words = sb.tile([P, width, PACK], BF16, name=name + "_words", align_bytes=64)
            codes = sb.tile([P, width], U32, name=name + "_codes", align_bytes=64)
            scales = sb.tile([P, width], U8, name=name + "_scales", align_bytes=64)
            return words, codes, scales

        def interleave(op, raw, raw0, col0, width, split):
            dst = op[0][:, col0 : col0 + width, :].rearrange("p (c i) j -> p c j i", i=RUN)
            src = raw[:, :, raw0 : raw0 + width].rearrange("p j (c i) -> p c j i", i=RUN)
            if split < width:
                nc.scalar.activation(out=dst[:, split // RUN :], in_=src[:, split // RUN :], func=ACT.Copy)
            if split > 0:
                nc.vector.tensor_copy(out=dst[:, : split // RUN], in_=src[:, : split // RUN])

        def quantize(op, col0, width):
            words, codes, scales = op
            cols = slice(col0, col0 + width)
            nc.vector.quantize_mx(out=codes[:, cols].bitcast(FP8X4), scales=scales[:, cols],
                                  in_=words[:, cols, :].rearrange("p c j -> p (c j)"))

        def products(acc, groups, weights, moving, c0, c1):
            for c in range(c0, c1, WIDTH):
                cols = slice(c, c + WIDTH)
                for g in groups:
                    nc.tensor.matmul_mx(out=acc[g][:, cols], lhsT=weights[1][rows(g), :].bitcast(FP8X4),
                                        lhsT_scale=weights[2][rows(g), :], rhs=moving[1][rows(g), cols].bitcast(FP8X4),
                                        rhs_scale=moving[2][rows(g), cols], start=True, stop=True)

        x_v = x.rearrange("g (p j) n -> (g p) j n", j=PACK)
        x_raw = [sb.tile([P, PACK, HALF], F32, name="x_raw%d" % h) for h in range(2)]
        w1_raw = sb.tile([P, PACK, M], F32)
        w2_raw = sb.tile([P, PACK, M], F32)
        wo_raw = sb.tile([P, PACK, O], F32)
        res_sb = sb.tile([P, G, N], F32)
        vec_rows = sb.tile([P, P], F32, align_bytes=64)
        vec_cols = sb.tile([P, P], F32, align_bytes=64)
        nc.vector.memset(vec_rows[:], 0.0)
        nc.sync.dma_start(out=x_raw[0][:], in_=x_v[:, :, 0:HALF])
        for r, vec in enumerate((tp, hs)):
            nc.sync.dma_start(out=vec_rows[r:P:ROWS, :].rearrange("q (g c) -> q g c", g=G),
                              in_=vec.rearrange("g (q c) o -> q g (c o)", c=ROWS))
        nc.sync.dma_start(out=w1_raw[:], in_=w1.rearrange("g (p j) m -> (g p) j m", j=PACK))
        nc.sync.dma_start(out=x_raw[1][:], in_=x_v[:, :, HALF:N])
        nc.sync.dma_start(out=w2_raw[:], in_=w2.rearrange("g (p j) m -> (g p) j m", j=PACK))
        nc.sync.dma_start(out=wo_raw[:], in_=wo2.rearrange("g (p j) o -> (g p) j o", j=PACK))
        nc.sync.dma_start(out=res_sb[:], in_=res.rearrange("g o n -> o g n"))

        delta = sb.tile([P, G, STEPS], F32)
        coef = sb.tile([P, G, STEPS], F32)
        nc.vector.memset(delta[:, :, 0:1], 0.0)
        for k in range(STEPS - 1):
            nc.vector.tensor_scalar(out=coef[:, :, k : k + 1], in0=delta[:, :, 0:1], scalar1=(-1.0) ** k / (STEPS - 1 - k),
                                    scalar2=None, op0=ALU.add)

        xq = packed("x", N)
        w1q = packed("w1", M)
        w2q = packed("w2", M)
        woq = packed("wo", O)
        hq = packed("h", N)

        neg_tp = sb.tile([P, G], F32)
        neg_half_hs = sb.tile([P, G], F32)
        z1 = [ps.tile([P, N], F32, name="z1_%d" % g) for g in range(G)]
        z2 = [ps.tile([P, N], F32, name="z2_%d" % g) for g in range(G)]

        neg_s = [sb.tile([P, N], F32, name="neg_s%d" % g) for g in range(G)]
        th = [sb.tile([P, N], F32, name="th%d" % g) for g in range(G)]
        gate = [sb.tile([P, N], F32, name="gate%d" % g) for g in range(G)]
        ex = [sb.tile([P, N], BF16, name="ex%d" % g) for g in range(G)]
        hh = [sb.tile([P, N], BF16, name="hh%d" % g) for g in range(G)]
        neg_max = sb.tile([P, G], F32)
        half_max = sb.tile([P, 2], F32)
        total = sb.tile([P, G], F32)
        guess = sb.tile([P, G], F32)
        inv = sb.tile([P, G], F32)
        shift = sb.tile([P, G, STEPS], F32)
        h_raw = sb.tile([P, PACK, N], BF16)

        def scores(g, c0, c1, so_far, minimum):
            nc.vector.tensor_scalar(out=neg_s[g][:, c0:c1], in0=z1[g][:, c0:c1], scalar1=neg_tp[:, g : g + 1], scalar2=so_far,
                                    op0=ALU.mult, op1=ALU.min, accum_out=minimum[:, g : g + 1])

        def exps(g):
            nc.scalar.activation(out=ex[g][:], in_=neg_s[g][:], func=ACT.Exp, scale=-1.0, bias=neg_max[:, g : g + 1],
                                 accum_out=total[:, g : g + 1])

        def tanh(g):
            nc.scalar.activation(out=th[g][:], in_=z2[g][:], func=ACT.Tanh, scale=0.5)

        def gates(g):
            nc.vector.tensor_scalar(out=gate[g][:], in0=th[g][:], scalar1=1.0, scalar2=neg_half_hs[:, g : g + 1],
                                    op0=ALU.add, op1=ALU.mult)

        def log_guess(g0, g1):
            bits = total[:, g0:g1].bitcast(U32)
            nc.scalar.activation(out=inv[:, g0:g1], in_=bits, func=ACT.Exp, scale=-GUESS_SLOPE, bias=GUESS_SHIFT)
            nc.scalar.activation(out=guess[:, g0:g1], in_=bits, func=ACT.Copy, scale=GUESS_SLOPE, bias=-GUESS_SHIFT)

        def log_delta(g0, g1):
            for g in range(g0, g1):
                nc.vector.tensor_scalar(out=delta[:, g, 1:STEPS], in0=total[:, g : g + 1].to_broadcast([P, STEPS - 1]),
                                        scalar1=inv[:, g : g + 1], scalar2=-1.0, op0=ALU.mult, op1=ALU.add)
            nc.vector.scalar_tensor_tensor(out=coef[:, g0:g1, STEPS - 1], in0=guess[:, g0:g1], scalar=-6.0,
                                           in1=neg_max[:, g0:g1], op0=ALU.add, op1=ALU.subtract)

        def log_series(g0, g1):
            flat = "p g s -> p (g s)"
            nc.vector.tensor_tensor_scan(out=shift[:, g0:g1, :].rearrange(flat), data0=delta[:, g0:g1, :].rearrange(flat),
                                         data1=coef[:, g0:g1, :].rearrange(flat), initial=0.0, op0=ALU.mult, op1=ALU.add)

        def hidden(g, c0, c1):
            nc.vector.scalar_tensor_tensor(out=hh[g][:, c0:c1], in0=neg_s[g][:, c0:c1], scalar=shift[:, g, STEPS - 1 : STEPS],
                                           in1=gate[g][:, c0:c1], op0=ALU.add, op1=ALU.mult)
            nc.sync.dma_start(out=h_raw[rows(g), :, c0:c1], in_=hh[g][:, c0:c1])

        interleave(xq, x_raw[0], 0, 0, HALF, 168)
        quantize(xq, 0, HALF)
        interleave(w1q, w1_raw, 0, 0, M, 64)
        nc.vector.transpose(out=vec_cols[:], in_=vec_rows[:])
        quantize(w1q, 0, M)
        nc.vector.tensor_scalar(out=neg_tp[:], in0=vec_cols[:, 0:P:ROWS], scalar1=-1.0, scalar2=None, op0=ALU.mult)
        nc.vector.tensor_scalar(out=neg_half_hs[:], in0=vec_cols[:, 1:P:ROWS], scalar1=-0.5, scalar2=None, op0=ALU.mult)
        products(z1, (0, 1), w1q, xq, 0, HALF)
        products(z1, (2, 3), w1q, xq, 0, HALF)
        interleave(xq, x_raw[1], 0, HALF, HALF, 168)
        scores(0, 0, HALF, None, half_max)
        quantize(xq, HALF, HALF)
        interleave(w2q, w2_raw, 0, 0, M, 64)
        scores(1, 0, HALF, None, half_max)
        quantize(w2q, 0, M)
        products(z1, (0, 2), w1q, xq, HALF, N)
        products(z1, (1, 3), w1q, xq, HALF, N)
        products(z2, (0, 1), w2q, xq, 0, N)
        products(z2, (2, 3), w2q, xq, 0, N)
        for g in range(2):
            scores(g, HALF, N, half_max[:, g : g + 1], neg_max)
        for g in range(2, G):
            scores(g, 0, N, None, neg_max)
        exps(0)
        exps(1)
        tanh(0)
        log_guess(0, 2)
        tanh(1)
        exps(2)
        exps(3)
        tanh(2)
        log_guess(2, 4)
        tanh(3)
        interleave(woq, wo_raw, 0, 0, O, 0)

        gates(0)
        log_delta(0, 2)
        gates(1)
        log_series(0, 2)
        hidden(0, 0, N)
        hidden(1, 0, N)
        log_delta(2, 4)
        gates(2)
        log_series(2, 4)
        gates(3)
        for c0 in (0, HALF):
            hidden(2, c0, c0 + HALF)
            hidden(3, c0, c0 + HALF)
        quantize(woq, 0, O)

        y = {0: [ps.tile([P, N], F32, name="z1_%d" % g) for g in range(G)],
             HALF: [ps.tile([P, N], F32, name="z2_%d" % g) for g in range(G)]}
        result = [sb.tile([P, N], F32, name="result%d" % g) for g in range(G)]
        for c0 in (0, HALF):
            interleave(hq, h_raw, c0, c0, HALF, 96 if c0 else 168)
            quantize(hq, c0, HALF)
            products(y[c0], (0, 1), woq, hq, c0, c0 + HALF)
            products(y[c0], (2, 3), woq, hq, c0, c0 + HALF)
        for c0 in (0, HALF):
            cols = slice(c0, c0 + HALF)
            for g in range(G):
                nc.vector.tensor_tensor(out=result[g][:, cols], in0=y[c0][g][:, cols], in1=res_sb[:, g, cols], op=ALU.add)
                nc.sync.dma_start(out=out[g, :, cols], in_=result[g][:, cols])
